import numpy as np
import ml_dtypes


def mxq(x, axis, fmt="e4m3"):
    dtype, down = {"e4m3": (ml_dtypes.float8_e4m3fn, 7), "e5m2": (ml_dtypes.float8_e5m2, 14)}[fmt]
    v = np.moveaxis(np.asarray(x, np.float32).astype(ml_dtypes.bfloat16).astype(np.float64), axis, -1)
    blocks = v.reshape(v.shape[:-1] + (-1, 32))
    amax = np.abs(blocks).max(-1, keepdims=True)
    byte = np.maximum(np.where(amax > 0, np.frexp(amax)[1] - 1 + 127, 0) - down, 1)
    scale = np.exp2(byte - 127.0)
    codes = (blocks / scale).astype(np.float32).astype(dtype).astype(np.float64)
    return np.moveaxis((codes * scale).reshape(v.shape), -1, axis)


WIDE = False


def mx_kscale(k):
    if not WIDE:
        return np.ones(k)
    levels = np.array([10, -10, 5, -5, 0])
    if k % 512:
        return np.exp2(np.random.permutation(np.resize(levels, k // 32))).repeat(32)
    a = np.empty((k // 512, 16))
    for p in range(k // 512):
        a[p, :8] = np.random.permutation(np.resize(levels, 8))
        for g in range(8):
            far = levels[np.abs(levels - a[p, g]) >= 10]
            a[p, g + 8] = far[np.random.randint(len(far))]
    return np.exp2(a.ravel()).repeat(32)


def f64(x):
    return np.asarray(x).astype(np.float64)


E2M1 = np.array([0.0, 0.5, 1.0, 1.5, 2.0, 3.0, 4.0, 6.0, -0.0, -0.5, -1.0, -1.5, -2.0, -3.0, -4.0, -6.0])


def pack_weight(w, fmt):
    k, n = w.shape
    w = f64(np.asarray(w, np.float32).astype(ml_dtypes.bfloat16)).reshape(k // 32, 32, n)
    amax = np.abs(w).max(1)
    if fmt == "e4m3":
        byte = np.frexp(amax)[1] - 1 + 127 - 7
    else:
        mant, ex = np.frexp(amax / 6.0)
        byte = np.where(mant > 0.5, ex, ex - 1) + 127
    byte = np.clip(np.where(amax > 0, byte, 1), 1, 254)
    scaled = (w * np.exp2(127.0 - byte)[:, None, :]).reshape(k, n).astype(np.float32)
    by_word = np.ascontiguousarray(scaled.reshape(k // 512, 128, 4, n).transpose(0, 1, 3, 2))
    if fmt == "e4m3":
        words = by_word.astype(ml_dtypes.float8_e4m3fn).view(np.uint8)
    else:
        c = by_word.astype(ml_dtypes.float4_e2m1fn).view(np.uint8) & 0xF
        words = (c[..., 0::2] | (c[..., 1::2] << 4)).reshape(k // 512, 128, 2 * n)
    return np.ascontiguousarray(words), np.ascontiguousarray(byte.astype(np.uint8).reshape(k // 512, 16, n))


def unpack_weight(words, scales, fmt):
    g, _, n = scales.shape
    words = np.ascontiguousarray(words).reshape(g, 128, n, -1)
    if fmt == "e4m3":
        vals = words.view(ml_dtypes.float8_e4m3fn).astype(np.float64)
    else:
        nib = np.empty((g, 128, n, 4), np.uint8)
        nib[..., 0::2] = words & 0xF
        nib[..., 1::2] = words >> 4
        vals = E2M1[nib]
    vals = vals * np.repeat(np.exp2(scales.astype(np.float64) - 127.0), 8, axis=1)[..., None]
    return vals.transpose(0, 1, 3, 2).reshape(g * 512, n)


K, T, R, N = 1024, 512, 512, 512


def setup_inputs():
    n = np.random.standard_normal
    fk = mx_kscale(K)
    fr = mx_kscale(R)
    xtp = pack_weight(n((K, T)) / fk[:, None], "e4m3")
    wap = pack_weight(n((K, R)) * 1 / np.sqrt(K) * fk[:, None] * fr, "e2m1")
    wcp = pack_weight(n((K, R)) * 1 / np.sqrt(K) * fk[:, None] * fr, "e4m3")
    wbp = pack_weight(n((R, N)) * 1 / np.sqrt(R) / fr[:, None], "e2m1")
    wyp = pack_weight(n((K, N)) * 1 / np.sqrt(K) * fk[:, None], "e4m3")
    return {
        "xt_words": xtp[0],
        "xt_scales": xtp[1],
        "wa_words": wap[0],
        "wa_scales": wap[1],
        "wc_words": wcp[0],
        "wc_scales": wcp[1],
        "wb_words": wbp[0],
        "wb_scales": wbp[1],
        "wy_words": wyp[0],
        "wy_scales": wyp[1],
    }


def reference(xt_words, xt_scales, wa_words, wa_scales, wc_words, wc_scales, wb_words, wb_scales, wy_words, wy_scales):
    xtu = unpack_weight(xt_words, xt_scales, "e4m3")
    wau = unpack_weight(wa_words, wa_scales, "e2m1")
    wcu = unpack_weight(wc_words, wc_scales, "e4m3")
    wbu = unpack_weight(wb_words, wb_scales, "e2m1")
    wyu = unpack_weight(wy_words, wy_scales, "e4m3")
    a = wau.T @ xtu
    b = wcu.T @ xtu
    hid = np.maximum(a, b)
    hidq = mxq(hid, 0, "e4m3")
    y = wbu.T @ hidq + wyu.T @ xtu
    return y

@@ -1,0 +1,237 @@
+from contextlib import ExitStack
+
+import concourse.mybir as mybir
+from concourse.masks import make_identity
+
+K, T, R, N = 1024, 512, 512, 512
+FLOPS = 2 * T * (2 * K * R + R * N + K * N)
+
+F32 = mybir.dt.float32
+BF16 = mybir.dt.bfloat16
+I32 = mybir.dt.int32
+U32 = mybir.dt.uint32
+U8 = mybir.dt.uint8
+FP8X4 = mybir.dt.float8_e4m3fn_x4
+FP4X4 = mybir.dt.float4_e2m1fn_x4
+
+P = 128
+PASSES = K // 512
+TILES = T // P
+HALF = T // 2
+WC_ROW = 4
+WY_ROW = 8
+WARM_PASSES = 16
+
+
+def tile_mix_hidden_larger_half_and_skip_kernel(
+    tc, xt_words, xt_scales, wa_words, wa_scales, wc_words, wc_scales, wb_words, wb_scales, wy_words, wy_scales, out
+):
+    nc = tc.nc
+    with ExitStack() as ctx:
+        keep = ctx.enter_context(tc.tile_pool(name="keep", bufs=1))
+        psum = ctx.enter_context(tc.psum_pool(name="psum", bufs=1))
+        ctx.enter_context(tc.manual_schedule())
+
+        def bank(index, name):
+            return psum.tile([P, 512], F32, name=name, tag="bank%d" % index)
+
+        xt = keep.tile([P, PASSES, T], U32, name="xt", align_bytes=64)
+        wc = keep.tile([P, PASSES, R], U32, name="wc", align_bytes=64)
+        wy = keep.tile([P, PASSES, N], U32, name="wy", align_bytes=64)
+        wa = keep.tile([P, PASSES, 2 * R], U8, name="wa", align_bytes=64)
+        wb = keep.tile([P, 1, 2 * N], U8, name="wb", align_bytes=64)
+        xt_s = keep.tile([P, PASSES, T], U8, name="xt_s", align_bytes=64)
+        wa_s = keep.tile([P, PASSES, R], U8, name="wa_s", align_bytes=64)
+        wc_s = keep.tile([P, PASSES, R], U8, name="wc_s", align_bytes=64)
+        wy_s = keep.tile([P, PASSES, N], U8, name="wy_s", align_bytes=64)
+        wb_s = keep.tile([P, 1, N], U8, name="wb_s", align_bytes=64)
+        ident = keep.tile([P, P], F32, name="ident", align_bytes=64)
+        warm_in = keep.tile([P, 512], BF16, name="warm_in", align_bytes=64)
+        warm_q = keep.tile([P, P], U32, name="warm_q", align_bytes=64)
+        warm_s = keep.tile([P, P], U8, name="warm_s", align_bytes=64)
+
+        def zero(plane):
+            nc.vector.memset(plane[:].bitcast(I32), 0)
+
+        zero(xt_s)
+        zero(wa_s)
+        nc.vector.memset(warm_in[:], 1.0)
+        zero(wc_s)
+        nc.vector.quantize_mx(out=warm_q[:].bitcast(FP8X4), scales=warm_s[:], in_=warm_in[:])
+        zero(wy_s)
+        zero(wb_s)
+        nc.vector.memset(ident[:], 0.0)
+        make_identity(nc, ident[:], nomemset=True)
+
+        def load_scale_rows(queue, plane, scales, r, first_row=0):
+            rows = scales.bitcast(I32).rearrange("z (q r) c -> r q z c", r=4)
+            queue.dma_start(out=plane[first_row + r : P : 32].bitcast(I32), in_=rows[r])
+
+        def load_e4m3(queue, tile, words):
+            queue.dma_start(out=tile[:].bitcast(I32), in_=words.rearrange("z p c r -> p z (c r)").bitcast(I32))
+
+        def load_e2m1(queue, tile, words):
+            queue.dma_start(out=tile[:].bitcast(I32), in_=words.rearrange("z p c -> p z c").bitcast(I32))
+
+        load_scale_rows(nc.sync, xt_s, xt_scales, 0)
+        load_scale_rows(nc.scalar, xt_s, xt_scales, 1)
+        load_scale_rows(nc.sync, xt_s, xt_scales, 2)
+        load_scale_rows(nc.scalar, xt_s, xt_scales, 3)
+        load_e4m3(nc.sync, xt, xt_words)
+        load_e2m1(nc.sync, wa, wa_words)
+        for r in range(4):
+            load_scale_rows(nc.scalar, wa_s, wa_scales, r)
+        load_e4m3(nc.sync, wc, wc_words)
+        for r in range(4):
+            load_scale_rows(nc.sync, wc_s, wc_scales, r, WC_ROW)
+        load_e4m3(nc.sync, wy, wy_words)
+        load_e2m1(nc.sync, wb, wb_words)
+        for r in range(4):
+            load_scale_rows(nc.sync, wy_s, wy_scales, r, WY_ROW)
+        for r in range(4):
+            load_scale_rows(nc.sync, wb_s, wb_scales, r)
+
+        warm_ps = bank(7, "warm_ps")
+        for i in range(WARM_PASSES):
+            nc.tensor.matmul_mx(
+                out=warm_ps[:, 0:P],
+                lhsT=warm_q[:].bitcast(FP8X4),
+                lhsT_scale=warm_s[:],
+                rhs=warm_q[:].bitcast(FP8X4),
+                rhs_scale=warm_s[:],
+                start=True,
+                stop=True,
+            )
+
+        def tokens(t):
+            return slice(t * P, (t + 1) * P)
+
+        def first_layer(ps, t, codes, plane):
+            for z in range(PASSES):
+                nc.tensor.matmul_mx(
+                    out=ps[:],
+                    lhsT=xt[:, z, tokens(t)].bitcast(FP8X4),
+                    lhsT_scale=xt_s[:, z, tokens(t)],
+                    rhs=codes(z),
+                    rhs_scale=plane(z),
+                    start=(z == 0),
+                    stop=(z == PASSES - 1),
+                )
+
+        def by_word(ps):
+            return ps[:].rearrange("t (p u e) -> t u p e", u=2, e=2)
+
+        def as_laid(sb):
+            return sb[:].rearrange("t (u p e) -> t u p e", u=2, e=2)
+
+        a_sb = []
+        for t in range(TILES):
+            a_ps = bank(t, "a_ps%d" % t)
+            first_layer(a_ps, t, lambda z: wa[:, z, :].bitcast(FP4X4), lambda z: wa_s[:, z, :])
+            sb = keep.tile([P, R], F32, name="a_sb%d" % t, align_bytes=64)
+            nc.scalar.copy(out=as_laid(sb), in_=by_word(a_ps))
+            a_sb.append(sb)
+
+        hid = []
+        for t in range(TILES):
+            b_ps = bank(4 + t, "b_ps%d" % t)
+            first_layer(b_ps, t, lambda z: wc[:, z, :].bitcast(FP8X4), lambda z: wc_s[WC_ROW:P, z, :])
+            sb = keep.tile([P, R], BF16, name="hid%d" % t, align_bytes=64)
+            nc.vector.tensor_tensor(out=as_laid(sb), in0=by_word(b_ps), in1=as_laid(a_sb[t]), op=mybir.AluOpType.max)
+            hid.append(sb)
+
+        hid_q = keep.tile([P, T], U32, name="hid_q", align_bytes=64)
+        hid_s = keep.tile([P, T], U8, name="hid_s", align_bytes=64)
+
+        def turn(ps, first_col, t):
+            for u in range(2):
+                col = first_col + u * P
+                nc.tensor.transpose(ps[:, col : col + P], hid[t][:].bitcast(F32)[:, u * P : (u + 1) * P], ident[:])
+
+        def regroup(copy, ps, count, name):
+            sb = keep.tile([P, count * 4 * P], BF16, name=name, align_bytes=64)
+            copy(
+                out=sb[:].bitcast(F32).rearrange("p (j t u) -> p j t u", j=count, u=2),
+                in_=ps[:, 0 : count * 2 * P].rearrange("p (j u t) -> p j t u", j=count, u=2),
+            )
+            return sb
+
+        def quantise(sb, first, count):
+            cols = slice(first * P, (first + count) * P)
+            nc.vector.quantize_mx(out=hid_q[:, cols].bitcast(FP8X4), scales=hid_s[:, cols], in_=sb[:])
+
+        def skip(ps, n_tiles, h):
+            cols = slice(h * HALF, (h + 1) * HALF)
+            for i, n in enumerate(n_tiles):
+                for z in range(PASSES):
+                    nc.tensor.matmul_mx(
+                        out=ps[:, i * HALF : (i + 1) * HALF],
+                        lhsT=wy[:, z, tokens(n)].bitcast(FP8X4),
+                        lhsT_scale=wy_s[WY_ROW:P, z, tokens(n)],
+                        rhs=xt[:, z, cols].bitcast(FP8X4),
+                        rhs_scale=xt_s[:, z, cols],
+                        start=(i == 0 and z == 0),
+                        stop=False,
+                    )
+
+        def second_layer(ps, n_tiles, h):
+            for i, n in enumerate(n_tiles):
+                for j in range(2):
+                    t = 2 * h + j
+                    col = i * HALF + j * P
+                    nc.tensor.matmul_mx(
+                        out=ps[:, col : col + P],
+                        lhsT=wb[:, 0, 2 * n * P : 2 * (n + 1) * P].bitcast(FP4X4),
+                        lhsT_scale=wb_s[:, 0, tokens(n)],
+                        rhs=hid_q[:, tokens(t)].bitcast(FP8X4),
+                        rhs_scale=hid_s[:, tokens(t)],
+                        start=False,
+                        stop=(i == len(n_tiles) - 1 and j == 1),
+                    )
+
+        def store(copy, queue, ps, n_tiles, h):
+            count = len(n_tiles)
+            sb = keep.tile([P, count * HALF], F32, name="out_sb%d_%d" % (h, n_tiles[0]), align_bytes=64)
+            copy(out=sb[:], in_=ps[:, 0 : count * HALF])
+            rows = out[n_tiles[0] * P : (n_tiles[0] + count) * P, h * HALF : (h + 1) * HALF]
+            queue.dma_start(
+                out=rows.rearrange("(i p) t -> p i t", p=P), in_=sb[:].rearrange("p (i t) -> p i t", i=count)
+            )
+
+        t01 = bank(0, "t01")
+        turn(t01, 0, 0)
+        turn(t01, 2 * P, 1)
+        g01 = regroup(nc.scalar.copy, t01, 2, "g01")
+        quantise(g01, 0, 2)
+
+        o00 = bank(3, "o00")
+        o01 = bank(4, "o01")
+        skip(o00, [0, 1], 0)
+        skip(o01, [2, 3], 0)
+
+        t2 = bank(1, "t2")
+        t3 = bank(2, "t3")
+        turn(t2, 0, 2)
+        turn(t3, 0, 3)
+        g2 = regroup(nc.scalar.copy, t2, 1, "g2")
+        g3 = regroup(nc.vector.tensor_copy, t3, 1, "g3")
+        quantise(g2, 2, 1)
+        quantise(g3, 3, 1)
+
+        second_layer(o00, [0, 1], 0)
+        store(nc.scalar.copy, nc.sync, o00, [0, 1], 0)
+        second_layer(o01, [2, 3], 0)
+        store(nc.vector.tensor_copy, nc.sync, o01, [2, 3], 0)
+
+        o10 = bank(5, "o10")
+        skip(o10, [0, 1], 1)
+        second_layer(o10, [0, 1], 1)
+        store(nc.scalar.copy, nc.sync, o10, [0, 1], 1)
+        o12 = bank(6, "o12")
+        skip(o12, [2], 1)
+        second_layer(o12, [2], 1)
+        store(nc.vector.tensor_copy, nc.sync, o12, [2], 1)
+        o13 = bank(7, "o13")
+        skip(o13, [3], 1)
+        second_layer(o13, [3], 1)
+        store(nc.scalar.copy, nc.scalar, o13, [3], 1)

@@ -35,7 +35,7 @@ def tile_mix_hidden_larger_half_and_skip_kernel(
         def bank(index, name):
             return psum.tile([P, 512], F32, name=name, tag="bank%d" % index)
 
-        xt = keep.tile([P, PASSES, T], U32, name="xt", align_bytes=64)
+        xt = [keep.tile([P, T], U32, name="xt%d" % z, align_bytes=64) for z in range(PASSES)]
         wc = keep.tile([P, PASSES, R], U32, name="wc", align_bytes=64)
         wy = keep.tile([P, PASSES, N], U32, name="wy", align_bytes=64)
         wa = keep.tile([P, PASSES, 2 * R], U8, name="wa", align_bytes=64)
@@ -70,6 +70,9 @@ def tile_mix_hidden_larger_half_and_skip_kernel(
         def load_e4m3(queue, tile, words):
             queue.dma_start(out=tile[:].bitcast(I32), in_=words.rearrange("z p c r -> p z (c r)").bitcast(I32))
 
+        def load_xt(z):
+            nc.sync.dma_start(out=xt[z][:].bitcast(I32), in_=xt_words[z].rearrange("p c r -> p (c r)").bitcast(I32))
+
         def load_e2m1(queue, tile, words):
             queue.dma_start(out=tile[:].bitcast(I32), in_=words.rearrange("z p c -> p z c").bitcast(I32))
 
@@ -77,10 +80,13 @@ def tile_mix_hidden_larger_half_and_skip_kernel(
         load_scale_rows(nc.scalar, xt_s, xt_scales, 1)
         load_scale_rows(nc.sync, xt_s, xt_scales, 2)
         load_scale_rows(nc.scalar, xt_s, xt_scales, 3)
-        load_e4m3(nc.sync, xt, xt_words)
+        load_xt(0)
         load_e2m1(nc.sync, wa, wa_words)
-        for r in range(4):
-            load_scale_rows(nc.scalar, wa_s, wa_scales, r)
+        load_scale_rows(nc.scalar, wa_s, wa_scales, 0)
+        load_scale_rows(nc.scalar, wa_s, wa_scales, 1)
+        load_scale_rows(nc.sync, wa_s, wa_scales, 2)
+        load_scale_rows(nc.sync, wa_s, wa_scales, 3)
+        load_xt(1)
         load_e4m3(nc.sync, wc, wc_words)
         for r in range(4):
             load_scale_rows(nc.sync, wc_s, wc_scales, r, WC_ROW)
@@ -106,11 +112,11 @@ def tile_mix_hidden_larger_half_and_skip_kernel(
         def tokens(t):
             return slice(t * P, (t + 1) * P)
 
-        def first_layer(ps, t, codes, plane):
-            for z in range(PASSES):
+        def first_layer(ps, t, codes, plane, passes):
+            for z in passes:
                 nc.tensor.matmul_mx(
                     out=ps[:],
-                    lhsT=xt[:, z, tokens(t)].bitcast(FP8X4),
+                    lhsT=xt[z][:, tokens(t)].bitcast(FP8X4),
                     lhsT_scale=xt_s[:, z, tokens(t)],
                     rhs=codes(z),
                     rhs_scale=plane(z),
@@ -125,17 +131,19 @@ def tile_mix_hidden_larger_half_and_skip_kernel(
             return sb[:].rearrange("t (u p e) -> t u p e", u=2, e=2)
 
         a_sb = []
+        a_ps = [bank(t, "a_ps%d" % t) for t in range(TILES)]
         for t in range(TILES):
-            a_ps = bank(t, "a_ps%d" % t)
-            first_layer(a_ps, t, lambda z: wa[:, z, :].bitcast(FP4X4), lambda z: wa_s[:, z, :])
+            first_layer(a_ps[t], t, lambda z: wa[:, z, :].bitcast(FP4X4), lambda z: wa_s[:, z, :], [0])
+        for t in range(TILES):
+            first_layer(a_ps[t], t, lambda z: wa[:, z, :].bitcast(FP4X4), lambda z: wa_s[:, z, :], [1])
             sb = keep.tile([P, R], F32, name="a_sb%d" % t, align_bytes=64)
-            nc.scalar.copy(out=as_laid(sb), in_=by_word(a_ps))
+            nc.scalar.copy(out=as_laid(sb), in_=by_word(a_ps[t]))
             a_sb.append(sb)
 
         hid = []
         for t in range(TILES):
             b_ps = bank(4 + t, "b_ps%d" % t)
-            first_layer(b_ps, t, lambda z: wc[:, z, :].bitcast(FP8X4), lambda z: wc_s[WC_ROW:P, z, :])
+            first_layer(b_ps, t, lambda z: wc[:, z, :].bitcast(FP8X4), lambda z: wc_s[WC_ROW:P, z, :], [0, 1])
             sb = keep.tile([P, R], BF16, name="hid%d" % t, align_bytes=64)
             nc.vector.tensor_tensor(out=as_laid(sb), in0=by_word(b_ps), in1=as_laid(a_sb[t]), op=mybir.AluOpType.max)
             hid.append(sb)
@@ -168,7 +176,7 @@ def tile_mix_hidden_larger_half_and_skip_kernel(
                         out=ps[:, i * HALF : (i + 1) * HALF],
                         lhsT=wy[:, z, tokens(n)].bitcast(FP8X4),
                         lhsT_scale=wy_s[WY_ROW:P, z, tokens(n)],
-                        rhs=xt[:, z, cols].bitcast(FP8X4),
+                        rhs=xt[z][:, cols].bitcast(FP8X4),
                         rhs_scale=xt_s[:, z, cols],
                         start=(i == 0 and z == 0),
                         stop=False,

@@ -168,57 +168,55 @@ def tile_mix_hidden_larger_half_and_skip_kernel(
             cols = slice(first * P, (first + count) * P)
             nc.vector.quantize_mx(out=hid_q[:, cols].bitcast(FP8X4), scales=hid_s[:, cols], in_=sb[:])
 
-        def skip(ps, n_tiles, h):
-            cols = slice(h * HALF, (h + 1) * HALF)
-            for i, n in enumerate(n_tiles):
-                for z in range(PASSES):
-                    nc.tensor.matmul_mx(
-                        out=ps[:, i * HALF : (i + 1) * HALF],
-                        lhsT=wy[:, z, tokens(n)].bitcast(FP8X4),
-                        lhsT_scale=wy_s[WY_ROW:P, z, tokens(n)],
-                        rhs=xt[z][:, cols].bitcast(FP8X4),
-                        rhs_scale=xt_s[:, z, cols],
-                        start=(i == 0 and z == 0),
-                        stop=False,
-                    )
+        def skip(ps, n, cols):
+            width = cols.stop - cols.start
+            for z in range(PASSES):
+                nc.tensor.matmul_mx(
+                    out=ps[:, 0:width],
+                    lhsT=wy[:, z, tokens(n)].bitcast(FP8X4),
+                    lhsT_scale=wy_s[WY_ROW:P, z, tokens(n)],
+                    rhs=xt[z][:, cols].bitcast(FP8X4),
+                    rhs_scale=xt_s[:, z, cols],
+                    start=(z == 0),
+                    stop=False,
+                )
 
-        def second_layer(ps, n_tiles, h):
-            for i, n in enumerate(n_tiles):
-                for j in range(2):
-                    t = 2 * h + j
-                    col = i * HALF + j * P
-                    nc.tensor.matmul_mx(
-                        out=ps[:, col : col + P],
-                        lhsT=wb[:, 0, 2 * n * P : 2 * (n + 1) * P].bitcast(FP4X4),
-                        lhsT_scale=wb_s[:, 0, tokens(n)],
-                        rhs=hid_q[:, tokens(t)].bitcast(FP8X4),
-                        rhs_scale=hid_s[:, tokens(t)],
-                        start=False,
-                        stop=(i == len(n_tiles) - 1 and j == 1),
-                    )
+        def second_layer(ps, n, cols):
+            for col in range(cols.start, cols.stop, P):
+                nc.tensor.matmul_mx(
+                    out=ps[:, col - cols.start : col - cols.start + P],
+                    lhsT=wb[:, 0, 2 * n * P : 2 * (n + 1) * P].bitcast(FP4X4),
+                    lhsT_scale=wb_s[:, 0, tokens(n)],
+                    rhs=hid_q[:, col : col + P].bitcast(FP8X4),
+                    rhs_scale=hid_s[:, col : col + P],
+                    start=False,
+                    stop=(col + P == cols.stop),
+                )
 
-        def store(copy, queue, ps, n_tiles, h):
-            count = len(n_tiles)
-            sb = keep.tile([P, count * HALF], F32, name="out_sb%d_%d" % (h, n_tiles[0]), align_bytes=64)
-            copy(out=sb[:], in_=ps[:, 0 : count * HALF])
-            rows = out[n_tiles[0] * P : (n_tiles[0] + count) * P, h * HALF : (h + 1) * HALF]
-            queue.dma_start(
-                out=rows.rearrange("(i p) t -> p i t", p=P), in_=sb[:].rearrange("p (i t) -> p i t", i=count)
-            )
+        def store(copy, queue, ps, n, cols):
+            width = cols.stop - cols.start
+            sb = keep.tile([P, width], F32, name="out_sb%d_%d" % (n, cols.start), align_bytes=64)
+            copy(out=sb[:], in_=ps[:, 0:width])
+            queue.dma_start(out=out[tokens(n), cols], in_=sb[:])
 
-        t01 = bank(0, "t01")
-        turn(t01, 0, 0)
-        turn(t01, 2 * P, 1)
-        g01 = regroup(nc.scalar.copy, t01, 2, "g01")
-        quantise(g01, 0, 2)
+        copies = [nc.scalar.copy, nc.vector.tensor_copy]
 
-        o00 = bank(3, "o00")
-        o01 = bank(4, "o01")
-        skip(o00, [0, 1], 0)
-        skip(o01, [2, 3], 0)
+        t0 = bank(0, "t0")
+        t1 = bank(1, "t1")
+        turn(t0, 0, 0)
+        turn(t1, 0, 1)
+        g0 = regroup(nc.scalar.copy, t0, 1, "g0")
+        g1 = regroup(nc.scalar.copy, t1, 1, "g1")
+        quantise(g0, 0, 1)
+        quantise(g1, 1, 1)
 
-        t2 = bank(1, "t2")
-        t3 = bank(2, "t3")
+        low = slice(0, HALF)
+        o_low = [bank(2 + n, "o_low%d" % n) for n in range(4)]
+        for n in range(4):
+            skip(o_low[n], n, low)
+
+        t2 = bank(0, "t2")
+        t3 = bank(1, "t3")
         turn(t2, 0, 2)
         turn(t3, 0, 3)
         g2 = regroup(nc.scalar.copy, t2, 1, "g2")
@@ -226,20 +224,13 @@ def tile_mix_hidden_larger_half_and_skip_kernel(
         quantise(g2, 2, 1)
         quantise(g3, 3, 1)
 
-        second_layer(o00, [0, 1], 0)
-        store(nc.scalar.copy, nc.sync, o00, [0, 1], 0)
-        second_layer(o01, [2, 3], 0)
-        store(nc.vector.tensor_copy, nc.sync, o01, [2, 3], 0)
+        for n in range(4):
+            second_layer(o_low[n], n, low)
+            store(copies[0 if n < 3 else 1], nc.sync, o_low[n], n, low)
 
-        o10 = bank(5, "o10")
-        skip(o10, [0, 1], 1)
-        second_layer(o10, [0, 1], 1)
-        store(nc.scalar.copy, nc.sync, o10, [0, 1], 1)
-        o12 = bank(6, "o12")
-        skip(o12, [2], 1)
-        second_layer(o12, [2], 1)
-        store(nc.vector.tensor_copy, nc.sync, o12, [2], 1)
-        o13 = bank(7, "o13")
-        skip(o13, [3], 1)
-        second_layer(o13, [3], 1)
-        store(nc.scalar.copy, nc.scalar, o13, [3], 1)
+        pieces = [(n, slice(HALF, T)) for n in range(3)] + [(3, tokens(2)), (3, tokens(3))]
+        for i, (n, cols) in enumerate(pieces):
+            ps = bank((6 + i) % 8, "o_high%d" % i)
+            skip(ps, n, cols)
+            second_layer(ps, n, cols)
+            store(copies[i % 2], nc.scalar if i == 4 else nc.sync, ps, n, cols)

from contextlib import ExitStack

import concourse.mybir as mybir
from concourse.masks import make_identity

K, T, R, N = 1024, 512, 512, 512
FLOPS = 2 * T * (2 * K * R + R * N + K * N)

F32 = mybir.dt.float32
BF16 = mybir.dt.bfloat16
I32 = mybir.dt.int32
U32 = mybir.dt.uint32
U8 = mybir.dt.uint8
FP8X4 = mybir.dt.float8_e4m3fn_x4
FP4X4 = mybir.dt.float4_e2m1fn_x4

P = 128
PASSES = K // 512
TILES = T // P
HALF = T // 2
WC_ROW = 4
WY_ROW = 8
WARM_PASSES = 16


def tile_mix_hidden_larger_half_and_skip_kernel(
    tc, xt_words, xt_scales, wa_words, wa_scales, wc_words, wc_scales, wb_words, wb_scales, wy_words, wy_scales, out
):
    nc = tc.nc
    with ExitStack() as ctx:
        keep = ctx.enter_context(tc.tile_pool(name="keep", bufs=1))
        psum = ctx.enter_context(tc.psum_pool(name="psum", bufs=1))
        ctx.enter_context(tc.manual_schedule())

        def bank(index, name):
            return psum.tile([P, 512], F32, name=name, tag="bank%d" % index)

        xt = [keep.tile([P, T], U32, name="xt%d" % z, align_bytes=64) for z in range(PASSES)]
        wc = keep.tile([P, PASSES, R], U32, name="wc", align_bytes=64)
        wy = keep.tile([P, PASSES, N], U32, name="wy", align_bytes=64)
        wa = keep.tile([P, PASSES, 2 * R], U8, name="wa", align_bytes=64)
        wb = keep.tile([P, 1, 2 * N], U8, name="wb", align_bytes=64)
        xt_s = keep.tile([P, PASSES, T], U8, name="xt_s", align_bytes=64)
        wa_s = keep.tile([P, PASSES, R], U8, name="wa_s", align_bytes=64)
        wc_s = keep.tile([P, PASSES, R], U8, name="wc_s", align_bytes=64)
        wy_s = keep.tile([P, PASSES, N], U8, name="wy_s", align_bytes=64)
        wb_s = keep.tile([P, 1, N], U8, name="wb_s", align_bytes=64)
        ident = keep.tile([P, P], F32, name="ident", align_bytes=64)
        warm_in = keep.tile([P, 512], BF16, name="warm_in", align_bytes=64)
        warm_q = keep.tile([P, P], U32, name="warm_q", align_bytes=64)
        warm_s = keep.tile([P, P], U8, name="warm_s", align_bytes=64)

        def zero(plane):
            nc.vector.memset(plane[:].bitcast(I32), 0)

        zero(xt_s)
        zero(wa_s)
        nc.vector.memset(warm_in[:], 1.0)
        zero(wc_s)
        nc.vector.quantize_mx(out=warm_q[:].bitcast(FP8X4), scales=warm_s[:], in_=warm_in[:])
        zero(wy_s)
        zero(wb_s)
        nc.vector.memset(ident[:], 0.0)
        make_identity(nc, ident[:], nomemset=True)

        def load_scale_rows(queue, plane, scales, r, first_row=0):
            rows = scales.bitcast(I32).rearrange("z (q r) c -> r q z c", r=4)
            queue.dma_start(out=plane[first_row + r : P : 32].bitcast(I32), in_=rows[r])

        def load_e4m3(queue, tile, words):
            queue.dma_start(out=tile[:].bitcast(I32), in_=words.rearrange("z p c r -> p z (c r)").bitcast(I32))

        def load_xt(z):
            nc.sync.dma_start(out=xt[z][:].bitcast(I32), in_=xt_words[z].rearrange("p c r -> p (c r)").bitcast(I32))

        def load_e2m1(queue, tile, words):
            queue.dma_start(out=tile[:].bitcast(I32), in_=words.rearrange("z p c -> p z c").bitcast(I32))

        load_scale_rows(nc.sync, xt_s, xt_scales, 0)
        load_scale_rows(nc.scalar, xt_s, xt_scales, 1)
        load_scale_rows(nc.sync, xt_s, xt_scales, 2)
        load_scale_rows(nc.scalar, xt_s, xt_scales, 3)
        load_xt(0)
        load_e2m1(nc.sync, wa, wa_words)
        load_scale_rows(nc.scalar, wa_s, wa_scales, 0)
        load_scale_rows(nc.scalar, wa_s, wa_scales, 1)
        load_scale_rows(nc.sync, wa_s, wa_scales, 2)
        load_scale_rows(nc.sync, wa_s, wa_scales, 3)
        load_xt(1)
        load_e4m3(nc.sync, wc, wc_words)
        for r in range(4):
            load_scale_rows(nc.sync, wc_s, wc_scales, r, WC_ROW)
        load_e4m3(nc.sync, wy, wy_words)
        load_e2m1(nc.sync, wb, wb_words)
        for r in range(4):
            load_scale_rows(nc.sync, wy_s, wy_scales, r, WY_ROW)
        for r in range(4):
            load_scale_rows(nc.sync, wb_s, wb_scales, r)

        warm_ps = bank(7, "warm_ps")
        for i in range(WARM_PASSES):
            nc.tensor.matmul_mx(
                out=warm_ps[:, 0:P],
                lhsT=warm_q[:].bitcast(FP8X4),
                lhsT_scale=warm_s[:],
                rhs=warm_q[:].bitcast(FP8X4),
                rhs_scale=warm_s[:],
                start=True,
                stop=True,
            )

        def tokens(t):
            return slice(t * P, (t + 1) * P)

        def first_layer(ps, t, codes, plane, passes):
            for z in passes:
                nc.tensor.matmul_mx(
                    out=ps[:],
                    lhsT=xt[z][:, tokens(t)].bitcast(FP8X4),
                    lhsT_scale=xt_s[:, z, tokens(t)],
                    rhs=codes(z),
                    rhs_scale=plane(z),
                    start=(z == 0),
                    stop=(z == PASSES - 1),
                )

        def by_word(ps):
            return ps[:].rearrange("t (p u e) -> t u p e", u=2, e=2)

        def as_laid(sb):
            return sb[:].rearrange("t (u p e) -> t u p e", u=2, e=2)

        a_sb = []
        a_ps = [bank(t, "a_ps%d" % t) for t in range(TILES)]
        for t in range(TILES):
            first_layer(a_ps[t], t, lambda z: wa[:, z, :].bitcast(FP4X4), lambda z: wa_s[:, z, :], [0])
        for t in range(TILES):
            first_layer(a_ps[t], t, lambda z: wa[:, z, :].bitcast(FP4X4), lambda z: wa_s[:, z, :], [1])
            sb = keep.tile([P, R], F32, name="a_sb%d" % t, align_bytes=64)
            nc.scalar.copy(out=as_laid(sb), in_=by_word(a_ps[t]))
            a_sb.append(sb)

        hid = []
        for t in range(TILES):
            b_ps = bank(4 + t, "b_ps%d" % t)
            first_layer(b_ps, t, lambda z: wc[:, z, :].bitcast(FP8X4), lambda z: wc_s[WC_ROW:P, z, :], [0, 1])
            sb = keep.tile([P, R], BF16, name="hid%d" % t, align_bytes=64)
            nc.vector.tensor_tensor(out=as_laid(sb), in0=by_word(b_ps), in1=as_laid(a_sb[t]), op=mybir.AluOpType.max)
            hid.append(sb)

        hid_q = keep.tile([P, T], U32, name="hid_q", align_bytes=64)
        hid_s = keep.tile([P, T], U8, name="hid_s", align_bytes=64)

        def turn(ps, first_col, t):
            for u in range(2):
                col = first_col + u * P
                nc.tensor.transpose(ps[:, col : col + P], hid[t][:].bitcast(F32)[:, u * P : (u + 1) * P], ident[:])

        def regroup(copy, ps, count, name):
            sb = keep.tile([P, count * 4 * P], BF16, name=name, align_bytes=64)
            copy(
                out=sb[:].bitcast(F32).rearrange("p (j t u) -> p j t u", j=count, u=2),
                in_=ps[:, 0 : count * 2 * P].rearrange("p (j u t) -> p j t u", j=count, u=2),
            )
            return sb

        def quantise(sb, first, count):
            cols = slice(first * P, (first + count) * P)
            nc.vector.quantize_mx(out=hid_q[:, cols].bitcast(FP8X4), scales=hid_s[:, cols], in_=sb[:])

        def skip(ps, n, cols):
            width = cols.stop - cols.start
            for z in range(PASSES):
                nc.tensor.matmul_mx(
                    out=ps[:, 0:width],
                    lhsT=wy[:, z, tokens(n)].bitcast(FP8X4),
                    lhsT_scale=wy_s[WY_ROW:P, z, tokens(n)],
                    rhs=xt[z][:, cols].bitcast(FP8X4),
                    rhs_scale=xt_s[:, z, cols],
                    start=(z == 0),
                    stop=False,
                )

        def second_layer(ps, n, cols):
            for col in range(cols.start, cols.stop, P):
                nc.tensor.matmul_mx(
                    out=ps[:, col - cols.start : col - cols.start + P],
                    lhsT=wb[:, 0, 2 * n * P : 2 * (n + 1) * P].bitcast(FP4X4),
                    lhsT_scale=wb_s[:, 0, tokens(n)],
                    rhs=hid_q[:, col : col + P].bitcast(FP8X4),
                    rhs_scale=hid_s[:, col : col + P],
                    start=False,
                    stop=(col + P == cols.stop),
                )

        def store(copy, queue, ps, n, cols):
            width = cols.stop - cols.start
            sb = keep.tile([P, width], F32, name="out_sb%d_%d" % (n, cols.start), align_bytes=64)
            copy(out=sb[:], in_=ps[:, 0:width])
            queue.dma_start(out=out[tokens(n), cols], in_=sb[:])

        copies = [nc.scalar.copy, nc.vector.tensor_copy]

        t0 = bank(0, "t0")
        t1 = bank(1, "t1")
        turn(t0, 0, 0)
        turn(t1, 0, 1)
        g0 = regroup(nc.scalar.copy, t0, 1, "g0")
        g1 = regroup(nc.scalar.copy, t1, 1, "g1")
        quantise(g0, 0, 1)
        quantise(g1, 1, 1)

        low = slice(0, HALF)
        o_low = [bank(2 + n, "o_low%d" % n) for n in range(4)]
        for n in range(4):
            skip(o_low[n], n, low)

        t2 = bank(0, "t2")
        t3 = bank(1, "t3")
        turn(t2, 0, 2)
        turn(t3, 0, 3)
        g2 = regroup(nc.scalar.copy, t2, 1, "g2")
        g3 = regroup(nc.vector.tensor_copy, t3, 1, "g3")
        quantise(g2, 2, 1)
        quantise(g3, 3, 1)

        for n in range(4):
            second_layer(o_low[n], n, low)
            store(copies[0 if n < 3 else 1], nc.sync, o_low[n], n, low)

        pieces = [(n, slice(HALF, T)) for n in range(3)] + [(3, tokens(2)), (3, tokens(3))]
        for i, (n, cols) in enumerate(pieces):
            ps = bank((6 + i) % 8, "o_high%d" % i)
            skip(ps, n, cols)
            second_layer(ps, n, cols)
            store(copies[i % 2], nc.scalar if i == 4 else nc.sync, ps, n, cols)
